import numpy as np
import ml_dtypes


def mxq(x, axis, fmt="e4m3"):
    dtype, down = {"e4m3": (ml_dtypes.float8_e4m3fn, 7), "e5m2": (ml_dtypes.float8_e5m2, 14)}[fmt]
    v = np.moveaxis(np.asarray(x, np.float32).astype(ml_dtypes.bfloat16).astype(np.float64), axis, -1)
    blocks = v.reshape(v.shape[:-1] + (-1, 32))
    amax = np.abs(blocks).max(-1, keepdims=True)
    byte = np.maximum(np.where(amax > 0, np.frexp(amax)[1] - 1 + 127, 0) - down, 1)
    scale = np.exp2(byte - 127.0)
    codes = (blocks / scale).astype(np.float32).astype(dtype).astype(np.float64)
    return np.moveaxis((codes * scale).reshape(v.shape), -1, axis)


WIDE = False


def mx_kscale(k):
    if not WIDE:
        return np.ones(k)
    levels = np.array([10, -10, 5, -5, 0])
    if k % 512:
        return np.exp2(np.random.permutation(np.resize(levels, k // 32))).repeat(32)
    a = np.empty((k // 512, 16))
    for p in range(k // 512):
        a[p, :8] = np.random.permutation(np.resize(levels, 8))
        for g in range(8):
            far = levels[np.abs(levels - a[p, g]) >= 10]
            a[p, g + 8] = far[np.random.randint(len(far))]
    return np.exp2(a.ravel()).repeat(32)


def f64(x):
    return np.asarray(x).astype(np.float64)


def striped(idx):
    return np.tile(idx.reshape(-1, 16).T, (8, 1)).astype(np.uint16)


def unstriped(offs):
    return offs[:16].T.reshape(-1).astype(np.int64)


E2M1 = np.array([0.0, 0.5, 1.0, 1.5, 2.0, 3.0, 4.0, 6.0, -0.0, -0.5, -1.0, -1.5, -2.0, -3.0, -4.0, -6.0])


def pack_weight(w, fmt):
    k, n = w.shape
    w = f64(np.asarray(w, np.float32).astype(ml_dtypes.bfloat16)).reshape(k // 32, 32, n)
    amax = np.abs(w).max(1)
    if fmt == "e4m3":
        byte = np.frexp(amax)[1] - 1 + 127 - 7
    else:
        mant, ex = np.frexp(amax / 6.0)
        byte = np.where(mant > 0.5, ex, ex - 1) + 127
    byte = np.clip(np.where(amax > 0, byte, 1), 1, 254)
    scaled = (w * np.exp2(127.0 - byte)[:, None, :]).reshape(k, n).astype(np.float32)
    by_word = np.ascontiguousarray(scaled.reshape(k // 512, 128, 4, n).transpose(0, 1, 3, 2))
    if fmt == "e4m3":
        words = by_word.astype(ml_dtypes.float8_e4m3fn).view(np.uint8)
    else:
        c = by_word.astype(ml_dtypes.float4_e2m1fn).view(np.uint8) & 0xF
        words = (c[..., 0::2] | (c[..., 1::2] << 4)).reshape(k // 512, 128, 2 * n)
    return np.ascontiguousarray(words), np.ascontiguousarray(byte.astype(np.uint8).reshape(k // 512, 16, n))


def unpack_weight(words, scales, fmt):
    g, _, n = scales.shape
    words = np.ascontiguousarray(words).reshape(g, 128, n, -1)
    if fmt == "e4m3":
        vals = words.view(ml_dtypes.float8_e4m3fn).astype(np.float64)
    else:
        nib = np.empty((g, 128, n, 4), np.uint8)
        nib[..., 0::2] = words & 0xF
        nib[..., 1::2] = words >> 4
        vals = E2M1[nib]
    vals = vals * np.repeat(np.exp2(scales.astype(np.float64) - 127.0), 8, axis=1)[..., None]
    return vals.transpose(0, 1, 3, 2).reshape(g * 512, n)


def relu2(v):
    return np.maximum(v, 0.0) ** 2


K, T, E, C, H, N = 1024, 512, 6, 256, 512, 256
TOP = 3


def by_expert(wq, xq):
    return np.concatenate([wq[e].T @ xq[:, e * C:(e + 1) * C] for e in range(E)], axis=1)


def setup_inputs():
    n = np.random.standard_normal
    s = mx_kscale(K)[:, None]
    u = mx_kscale(H)
    deal = np.repeat(np.arange(E), C).reshape(TOP, T)[:, np.random.permutation(T)]
    deal = np.take_along_axis(deal, np.argsort(np.random.rand(TOP, T), axis=0), axis=0)
    for _ in range(8):
        s_, t_ = np.random.permutation(T).reshape(2, -1); r = np.random.randint(TOP, size=T // 2); x, y = deal[r, s_].copy(), deal[r, t_].copy()
        ok = ~((deal[:, s_] == y).any(0) | (deal[:, t_] == x).any(0)); deal[r[ok], s_[ok]] = y[ok]; deal[r[ok], t_[ok]] = x[ok]
    order = np.lexsort((np.random.rand(TOP * T), deal.reshape(-1)))
    slot_token = order % T; pos = np.empty(TOP * T, np.int64); pos[order] = np.arange(TOP * T); pos = pos.reshape(TOP, T)
    g = np.random.uniform(0.5, 1.5, (TOP, T)); g = g / g.sum(0)
    x = pack_weight(n((K, T)) * s, "e4m3")
    return {
        "x_words": x[0],
        "x_scales": x[1],
        "w1": (n((E, K, H)) / np.sqrt(K) / s[None] * u[None, None, :]).astype(np.float32),
        "w2": (n((E, H, N)) / np.sqrt(H) / u[None, :, None] ** 2).astype(np.float32),
        "gate": np.stack([np.tile(r, (N, 1)) for r in g]).astype(np.float32),
        "offs": striped(slot_token),
        "pos1": striped(pos[0]),
        "pos2": striped(pos[1]),
        "pos3": striped(pos[2]),
    }


def reference(x_words, x_scales, w1, w2, gate, offs, pos1, pos2, pos3):
    idx = unstriped(offs)
    xq = unpack_weight(x_words, x_scales, "e4m3")[:, idx]
    h = relu2(by_expert(mxq(f64(w1), 1, "e4m3"), xq))
    y = by_expert(mxq(f64(w2), 1, "e4m3"), mxq(h, 0, "e4m3"))
    return sum(f64(gate[r]) * y[:, unstriped(p)] for r, p in enumerate((pos1, pos2, pos3)))

@@ -1,0 +1,232 @@
+from contextlib import ExitStack
+
+import concourse.mybir as mybir
+from concourse.masks import make_identity
+
+K, T, E, C, H, N = 1024, 512, 6, 256, 512, 256
+TOP = 3
+S = E * C
+P = 128
+PACK = 4
+K_PASS = P * PACK
+PASSES = K // K_PASS
+BLOCKS = N // P
+HALVES = C // P
+LIST_COLS = C // 16
+TURNED = TOP - 1
+TOKEN_BLOCKS = T // P
+AHEAD = 3
+SCALAR_ALONE = 2
+VECTOR_SHARE = 48
+LATE_ON_VECTOR = 4
+
+FLOPS = 2 * S * (K * H + H * N)
+BYTES = 4 * E * (K * H + H * N) + K * T + K * T // 32 + 4 * TOP * T + 2 * P * (S + TOP * T) // 16 + 4 * N * T
+
+F32 = mybir.dt.float32
+BF16 = mybir.dt.bfloat16
+I32 = mybir.dt.int32
+U32 = mybir.dt.uint32
+U16 = mybir.dt.uint16
+U8 = mybir.dt.uint8
+FP8X4 = mybir.dt.float8_e4m3fn_x4
+ACT = mybir.ActivationFunctionType
+MULT = mybir.AluOpType.mult
+ADD = mybir.AluOpType.add
+
+
+def tile_moe_pkd_mlp_relu2_kernel(tc, x_words, x_scales, w1, w2, gate, offs, pos1, pos2, pos3, out):
+    nc = tc.nc
+    with ExitStack() as ctx:
+        keep = ctx.enter_context(tc.tile_pool(name="keep", bufs=1))
+        ring = ctx.enter_context(tc.tile_pool(name="ring", bufs=3))
+        psum_a = ctx.enter_context(tc.psum_pool(name="psum_a", bufs=5))
+        psum_y = ctx.enter_context(tc.psum_pool(name="psum_y", bufs=3))
+
+        offs_t = keep.tile([P, S // 16], U16, name="offs_t")
+        pos_t = [keep.tile([P, T // 16], U16, name=f"pos_t{r}") for r in range(TOP)]
+        xw = [keep.tile([P, T], I32, name=f"xw{o}", align_bytes=64) for o in range(PASSES)]
+        xs = keep.tile([P, T], U8, name="xs", align_bytes=64)
+        w1_raw = [[keep.tile([P, PACK, H], F32, name=f"w1_raw{e}_{o}", align_bytes=64) for o in range(PASSES)] for e in range(E)]
+        w2_raw = [[keep.tile([P, PACK, P], F32, name=f"w2_raw{e}_{b}") for b in range(BLOCKS)] for e in range(E)]
+        gate_last = keep.tile([P, T], F32, name="gate_last")
+        gate_rows = keep.tile([P, P], F32, name="gate_rows")
+        gate_cols = keep.tile([P, TURNED * TOKEN_BLOCKS], F32, name="gate_cols")
+        identity = keep.tile([P, P], F32, name="identity")
+        y = [keep.tile([P, S], F32, name=f"y{b}") for b in range(BLOCKS)]
+        h_codes = [keep.tile([P, C], U32, name=f"h_codes{e}", align_bytes=64) for e in range(E)]
+        h_scales = [keep.tile([P, C], U8, name=f"h_scales{e}", align_bytes=64) for e in range(E)]
+        xg = {}
+        xsg = {}
+
+        def load_w1(e, o):
+            rows = w1[e, o * K_PASS:(o + 1) * K_PASS, :]
+            nc.sync.dma_start(out=w1_raw[e][o][:], in_=rows.rearrange("(p j) c -> p j c", j=PACK))
+
+        def load_w2(e, b):
+            rows = w2[e, :, b * P:(b + 1) * P]
+            nc.sync.dma_start(out=w2_raw[e][b][:], in_=rows.rearrange("(p j) c -> p j c", j=PACK))
+
+        def load_words(o):
+            nc.sync.dma_start(out=xw[o][:], in_=x_words[o].rearrange("p t r -> p (t r)").bitcast(I32))
+
+        nc.vector.memset(xs[:].bitcast(I32), 0)
+        nc.gpsimd.memset(gate_rows[:], 0.0)
+        make_identity(nc, identity[:])
+        nc.sync.dma_start(offs_t[:], offs)
+        load_words(0)
+        load_words(1)
+        load_w1(0, 0)
+        for q in range(4):
+            nc.sync.dma_start(out=xs[32 * q:32 * q + 4 * PASSES, :].bitcast(I32),
+                              in_=x_scales[:, 4 * q:4 * q + 4, :].bitcast(I32))
+        load_w1(0, 1)
+        for e in range(1, E):
+            load_w1(e, 0)
+            load_w1(e, 1)
+        for r, pos in enumerate((pos1, pos2, pos3)):
+            nc.sync.dma_start(pos_t[r][:], pos)
+        nc.sync.dma_start(out=gate_rows[0:TURNED * TOKEN_BLOCKS, :],
+                          in_=gate[0:TURNED, 0, :].rearrange("r (j p) -> r j p", p=P))
+        for e in range(E):
+            load_w2(e, 0)
+        for e in range(E):
+            load_w2(e, 1)
+        nc.sync.dma_start(out=gate_last[:], in_=gate[TOP - 1, 0:P, :])
+
+        def gather_words(e):
+            cols = offs_t[:, e * LIST_COLS:(e + 1) * LIST_COLS]
+            tag = f"xg{e}" if e < AHEAD else f"w1_raw{e - AHEAD}_0"
+            xg[e] = keep.tile([P, PASSES, C], U32, name=f"xg{e}", tag=tag, align_bytes=64)
+            for o in range(PASSES):
+                nc.vector.tensor_copy(xg[e][:, o, :], xw[o][:].bitcast(U32).indirect(cols))
+
+        def gather_scales(e):
+            cols = offs_t[:, e * LIST_COLS:(e + 1) * LIST_COLS]
+            xsg[e] = keep.tile([P, C], U8, name=f"xsg{e}", align_bytes=64)
+            nc.vector.tensor_copy(xsg[e][:], xs[:].indirect(cols))
+
+        def copy_on(engine, dst, src):
+            if engine == "vector":
+                nc.vector.tensor_copy(out=dst, in_=src)
+            else:
+                nc.scalar.copy(out=dst, in_=src)
+
+        def cast_w1(e, o):
+            grouped = ring.tile([P, H * PACK], BF16, name=f"w1_bf{o}", align_bytes=64)
+            dst = grouped[:].rearrange("p (t m j) -> p m j t", t=PACK, j=PACK)
+            src = w1_raw[e][o][:].rearrange("p j (m t) -> p m j t", t=PACK)
+            split = 0 if e < SCALAR_ALONE else (P, VECTOR_SHARE)[o]
+            if split > 0:
+                nc.vector.tensor_copy(out=dst[:, 0:split], in_=src[:, 0:split])
+            if split < P:
+                nc.scalar.copy(out=dst[:, split:P], in_=src[:, split:P])
+            return grouped
+
+        def cast_w2(e, b, engine):
+            grouped = ring.tile([P, P * PACK], BF16, name=f"w2_bf_{engine}", align_bytes=64)
+            copy_on(engine,
+                    grouped[:].rearrange("p (c i j) -> p c j i", i=PACK, j=PACK),
+                    w2_raw[e][b][:].rearrange("p j (c i) -> p c j i", i=PACK))
+            return grouped
+
+        def quantize(grouped, width, name):
+            codes = ring.tile([P, width], U32, name=f"{name}_codes", align_bytes=64, bufs=2)
+            scales = ring.tile([P, width], U8, name=f"{name}_scales", align_bytes=64, bufs=2)
+            nc.vector.quantize_mx(out=codes[:].bitcast(FP8X4), scales=scales[:], in_=grouped[:])
+            return codes, scales
+
+        def first_layer(e, w1_mx):
+            h_bf = ring.tile([P, C * PACK], BF16, name="h_bf", align_bytes=64)
+            tag = f"w1_raw{e + 1}_1" if e + 1 < E else "relu_last"
+            relu = keep.tile([P, HALVES, P, PACK], F32, name=f"relu{e}", tag=tag, align_bytes=64)
+            for half in range(HALVES):
+                slots = slice(half * P, (half + 1) * P)
+                a = psum_a.tile([P, PACK, P], F32, name="a")
+                for t in range(PACK):
+                    cols = slice(t * P, (t + 1) * P)
+                    for o in range(PASSES):
+                        codes, scales = w1_mx[o]
+                        nc.tensor.matmul_mx(out=a[:, t, :], lhsT=codes[:, cols].bitcast(FP8X4), lhsT_scale=scales[:, cols],
+                                            rhs=xg[e][:, o, slots].bitcast(FP8X4), rhs_scale=xsg[e][4 * o:P, slots],
+                                            start=(o == 0), stop=(o == PASSES - 1))
+                nc.scalar.activation(out=relu[:, half], in_=a[:].rearrange("p t s -> p s t"), func=ACT.Relu)
+                nc.scalar.activation(out=h_bf[:, half * P * PACK:(half + 1) * P * PACK],
+                                     in_=relu[:, half].rearrange("p s t -> p (s t)"), func=ACT.Square)
+            return h_bf
+
+        acc = {}
+
+        def second_layer(e, b, w2_mx):
+            codes, scales = w2_mx
+            if e % 2 == 0:
+                acc[b] = psum_y.tile([P, 2, C], F32, name="acc")
+            nc.tensor.matmul_mx(out=acc[b][:, e % 2, :], lhsT=codes[:].bitcast(FP8X4), lhsT_scale=scales[:],
+                                rhs=h_codes[e][:].bitcast(FP8X4), rhs_scale=h_scales[e][:], start=True, stop=True)
+            if e % 2 == 1:
+                nc.scalar.copy(out=y[b][:, (e - 1) * C:(e + 1) * C], in_=acc[b][:].rearrange("p x c -> p (x c)"))
+
+        def turn_gates():
+            turned = psum_a.tile([P, PACK, P], F32, name="a")
+            nc.tensor.transpose(turned[:, 0, :], gate_rows[:], identity[:])
+            nc.scalar.copy(out=gate_cols[:], in_=turned[:, 0, 0:TURNED * TOKEN_BLOCKS])
+
+        def combine(b):
+            scaled = []
+            for r in range(TURNED):
+                picked = keep.tile([P, T], F32, name=f"picked{b}_{r}", tag=f"w2_raw{3 + 2 * r}_1" if b == 0 else f"w2_raw{r}_0")
+                nc.vector.tensor_copy(picked[:], y[b][:].indirect(pos_t[r][:]))
+                turned = psum_a.tile([P, TOKEN_BLOCKS, P], F32, name="a")
+                term = ring.tile([P, TOKEN_BLOCKS, P], F32, name="term", bufs=4)
+                for j in range(TOKEN_BLOCKS):
+                    nc.tensor.transpose(turned[:, j, :], picked[:, j * P:(j + 1) * P], identity[:])
+                for j in range(TOKEN_BLOCKS):
+                    col = r * TOKEN_BLOCKS + j
+                    nc.scalar.activation(out=term[:, j, :], in_=turned[:, j, :], func=ACT.Copy,
+                                         scale=gate_cols[:, col:col + 1])
+                scaled.append(term)
+            last = keep.tile([P, T], F32, name=f"last{b}", tag="w2_raw4_1" if b == 0 else "w2_raw2_0")
+            nc.vector.tensor_tensor(last[:], y[b][:].indirect(pos_t[TOP - 1][:]), gate_last[:], MULT)
+            partial = psum_a.tile([P, TOKEN_BLOCKS, P], F32, name="a")
+            for j in range(TOKEN_BLOCKS):
+                for r in range(TURNED):
+                    nc.tensor.matmul(partial[:, j, :], lhsT=scaled[r][:, j, :], rhs=identity[:], is_transpose=True,
+                                     start=(r == 0), stop=(r == TURNED - 1))
+            return partial, last
+
+        def finish(b, partial, last):
+            total = keep.tile([P, T], F32, name=f"total{b}", tag=f"w2_raw{TURNED - 1 - b}_0")
+            nc.vector.tensor_tensor(total[:], partial[:].rearrange("p j t -> p (j t)"), last[:], ADD)
+            nc.sync.dma_start(out=out[b * P:(b + 1) * P, :], in_=total[:])
+
+        h_bf = {}
+
+        def quantize_h(e):
+            nc.vector.quantize_mx(out=h_codes[e][:].bitcast(FP8X4), scales=h_scales[e][:], in_=h_bf[e][:])
+
+        for e in range(E):
+            if e < AHEAD:
+                gather_words(e)
+            gather_scales(e)
+        w1_bf = [cast_w1(0, o) for o in range(PASSES)]
+        for e in range(E):
+            w1_mx = [quantize(w1_bf[o], H, f"w1_{o}") for o in range(PASSES)]
+            if e + AHEAD < E:
+                gather_words(e + AHEAD)
+            if e > 0:
+                quantize_h(e - 1)
+            if e + 1 < E:
+                w1_bf = [cast_w1(e + 1, o) for o in range(PASSES)]
+            h_bf[e] = first_layer(e, w1_mx)
+        turn_gates()
+        w2_bf = [cast_w2(e, 0, "vector") for e in range(2)]
+        quantize_h(E - 1)
+        for e in range(E):
+            if e + 2 < E:
+                w2_bf.append(cast_w2(e + 2, 0, "vector"))
+            second_layer(e, 0, quantize(w2_bf[e], P, "w2a"))
+        for e in range(E):
+            second_layer(e, 1, quantize(cast_w2(e, 1, "scalar" if e >= LATE_ON_VECTOR else "vector"), P, "w2b"))
+        parts = [combine(b) for b in range(BLOCKS)]
+        for b in range(BLOCKS):
+            finish(b, *parts[b])

@@ -18,7 +18,6 @@ TOKEN_BLOCKS = T // P
 AHEAD = 3
 SCALAR_ALONE = 2
 VECTOR_SHARE = 48
-LATE_ON_VECTOR = 4
 
 FLOPS = 2 * S * (K * H + H * N)
 BYTES = 4 * E * (K * H + H * N) + K * T + K * T // 32 + 4 * TOP * T + 2 * P * (S + TOP * T) // 16 + 4 * N * T
@@ -40,15 +39,14 @@ def tile_moe_pkd_mlp_relu2_kernel(tc, x_words, x_scales, w1, w2, gate, offs, pos
     with ExitStack() as ctx:
         keep = ctx.enter_context(tc.tile_pool(name="keep", bufs=1))
         ring = ctx.enter_context(tc.tile_pool(name="ring", bufs=3))
-        psum_a = ctx.enter_context(tc.psum_pool(name="psum_a", bufs=5))
-        psum_y = ctx.enter_context(tc.psum_pool(name="psum_y", bufs=3))
+        psum_a = ctx.enter_context(tc.psum_pool(name="psum_a", bufs=8))
 
         offs_t = keep.tile([P, S // 16], U16, name="offs_t")
         pos_t = [keep.tile([P, T // 16], U16, name=f"pos_t{r}") for r in range(TOP)]
         xw = [keep.tile([P, T], I32, name=f"xw{o}", align_bytes=64) for o in range(PASSES)]
         xs = keep.tile([P, T], U8, name="xs", align_bytes=64)
         w1_raw = [[keep.tile([P, PACK, H], F32, name=f"w1_raw{e}_{o}", align_bytes=64) for o in range(PASSES)] for e in range(E)]
-        w2_raw = [[keep.tile([P, PACK, P], F32, name=f"w2_raw{e}_{b}") for b in range(BLOCKS)] for e in range(E)]
+        w2_raw = [keep.tile([P, PACK, N], F32, name=f"w2_raw{e}") for e in range(E)]
         gate_last = keep.tile([P, T], F32, name="gate_last")
         gate_rows = keep.tile([P, P], F32, name="gate_rows")
         gate_cols = keep.tile([P, TURNED * TOKEN_BLOCKS], F32, name="gate_cols")
@@ -63,9 +61,8 @@ def tile_moe_pkd_mlp_relu2_kernel(tc, x_words, x_scales, w1, w2, gate, offs, pos
             rows = w1[e, o * K_PASS:(o + 1) * K_PASS, :]
             nc.sync.dma_start(out=w1_raw[e][o][:], in_=rows.rearrange("(p j) c -> p j c", j=PACK))
 
-        def load_w2(e, b):
-            rows = w2[e, :, b * P:(b + 1) * P]
-            nc.sync.dma_start(out=w2_raw[e][b][:], in_=rows.rearrange("(p j) c -> p j c", j=PACK))
+        def load_w2(e):
+            nc.sync.dma_start(out=w2_raw[e][:], in_=w2[e].rearrange("(p j) c -> p j c", j=PACK))
 
         def load_words(o):
             nc.sync.dma_start(out=xw[o][:], in_=x_words[o].rearrange("p t r -> p (t r)").bitcast(I32))
@@ -84,14 +81,12 @@ def tile_moe_pkd_mlp_relu2_kernel(tc, x_words, x_scales, w1, w2, gate, offs, pos
         for e in range(1, E):
             load_w1(e, 0)
             load_w1(e, 1)
+        for e in range(E):
+            load_w2(e)
         for r, pos in enumerate((pos1, pos2, pos3)):
             nc.sync.dma_start(pos_t[r][:], pos)
         nc.sync.dma_start(out=gate_rows[0:TURNED * TOKEN_BLOCKS, :],
                           in_=gate[0:TURNED, 0, :].rearrange("r (j p) -> r j p", p=P))
-        for e in range(E):
-            load_w2(e, 0)
-        for e in range(E):
-            load_w2(e, 1)
         nc.sync.dma_start(out=gate_last[:], in_=gate[TOP - 1, 0:P, :])
 
         def gather_words(e):
@@ -106,12 +101,6 @@ def tile_moe_pkd_mlp_relu2_kernel(tc, x_words, x_scales, w1, w2, gate, offs, pos
             xsg[e] = keep.tile([P, C], U8, name=f"xsg{e}", align_bytes=64)
             nc.vector.tensor_copy(xsg[e][:], xs[:].indirect(cols))
 
-        def copy_on(engine, dst, src):
-            if engine == "vector":
-                nc.vector.tensor_copy(out=dst, in_=src)
-            else:
-                nc.scalar.copy(out=dst, in_=src)
-
         def cast_w1(e, o):
             grouped = ring.tile([P, H * PACK], BF16, name=f"w1_bf{o}", align_bytes=64)
             dst = grouped[:].rearrange("p (t m j) -> p m j t", t=PACK, j=PACK)
@@ -123,16 +112,15 @@ def tile_moe_pkd_mlp_relu2_kernel(tc, x_words, x_scales, w1, w2, gate, offs, pos
                 nc.scalar.copy(out=dst[:, split:P], in_=src[:, split:P])
             return grouped
 
-        def cast_w2(e, b, engine):
-            grouped = ring.tile([P, P * PACK], BF16, name=f"w2_bf_{engine}", align_bytes=64)
-            copy_on(engine,
-                    grouped[:].rearrange("p (c i j) -> p c j i", i=PACK, j=PACK),
-                    w2_raw[e][b][:].rearrange("p j (c i) -> p c j i", i=PACK))
+        def cast_w2(e):
+            grouped = ring.tile([P, N * PACK], BF16, name="w2_bf", align_bytes=64)
+            nc.vector.tensor_copy(out=grouped[:].rearrange("p (c i j) -> p c j i", i=PACK, j=PACK),
+                                  in_=w2_raw[e][:].rearrange("p j (c i) -> p c j i", i=PACK))
             return grouped
 
-        def quantize(grouped, width, name):
-            codes = ring.tile([P, width], U32, name=f"{name}_codes", align_bytes=64, bufs=2)
-            scales = ring.tile([P, width], U8, name=f"{name}_scales", align_bytes=64, bufs=2)
+        def quantize(grouped, width, name, bufs):
+            codes = ring.tile([P, width], U32, name=f"{name}_codes", align_bytes=64, bufs=bufs)
+            scales = ring.tile([P, width], U8, name=f"{name}_scales", align_bytes=64, bufs=bufs)
             nc.vector.quantize_mx(out=codes[:].bitcast(FP8X4), scales=scales[:], in_=grouped[:])
             return codes, scales
 
@@ -155,16 +143,15 @@ def tile_moe_pkd_mlp_relu2_kernel(tc, x_words, x_scales, w1, w2, gate, offs, pos
                                      in_=relu[:, half].rearrange("p s t -> p (s t)"), func=ACT.Square)
             return h_bf
 
-        acc = {}
-
-        def second_layer(e, b, w2_mx):
+        def second_layer(e, w2_mx):
             codes, scales = w2_mx
-            if e % 2 == 0:
-                acc[b] = psum_y.tile([P, 2, C], F32, name="acc")
-            nc.tensor.matmul_mx(out=acc[b][:, e % 2, :], lhsT=codes[:].bitcast(FP8X4), lhsT_scale=scales[:],
-                                rhs=h_codes[e][:].bitcast(FP8X4), rhs_scale=h_scales[e][:], start=True, stop=True)
-            if e % 2 == 1:
-                nc.scalar.copy(out=y[b][:, (e - 1) * C:(e + 1) * C], in_=acc[b][:].rearrange("p x c -> p (x c)"))
+            acc = psum_a.tile([P, BLOCKS, C], F32, name="a")
+            for b in range(BLOCKS):
+                cols = slice(b * P, (b + 1) * P)
+                nc.tensor.matmul_mx(out=acc[:, b, :], lhsT=codes[:, cols].bitcast(FP8X4), lhsT_scale=scales[:, cols],
+                                    rhs=h_codes[e][:].bitcast(FP8X4), rhs_scale=h_scales[e][:], start=True, stop=True)
+            for b in range(BLOCKS):
+                nc.scalar.copy(out=y[b][:, e * C:(e + 1) * C], in_=acc[:, b, :])
 
         def turn_gates():
             turned = psum_a.tile([P, PACK, P], F32, name="a")
@@ -174,7 +161,7 @@ def tile_moe_pkd_mlp_relu2_kernel(tc, x_words, x_scales, w1, w2, gate, offs, pos
         def combine(b):
             scaled = []
             for r in range(TURNED):
-                picked = keep.tile([P, T], F32, name=f"picked{b}_{r}", tag=f"w2_raw{3 + 2 * r}_1" if b == 0 else f"w2_raw{r}_0")
+                picked = keep.tile([P, T], F32, name=f"picked{b}_{r}")
                 nc.vector.tensor_copy(picked[:], y[b][:].indirect(pos_t[r][:]))
                 turned = psum_a.tile([P, TOKEN_BLOCKS, P], F32, name="a")
                 term = ring.tile([P, TOKEN_BLOCKS, P], F32, name="term", bufs=4)
@@ -185,7 +172,7 @@ def tile_moe_pkd_mlp_relu2_kernel(tc, x_words, x_scales, w1, w2, gate, offs, pos
                     nc.scalar.activation(out=term[:, j, :], in_=turned[:, j, :], func=ACT.Copy,
                                          scale=gate_cols[:, col:col + 1])
                 scaled.append(term)
-            last = keep.tile([P, T], F32, name=f"last{b}", tag="w2_raw4_1" if b == 0 else "w2_raw2_0")
+            last = keep.tile([P, T], F32, name=f"last{b}")
             nc.vector.tensor_tensor(last[:], y[b][:].indirect(pos_t[TOP - 1][:]), gate_last[:], MULT)
             partial = psum_a.tile([P, TOKEN_BLOCKS, P], F32, name="a")
             for j in range(TOKEN_BLOCKS):
@@ -195,7 +182,7 @@ def tile_moe_pkd_mlp_relu2_kernel(tc, x_words, x_scales, w1, w2, gate, offs, pos
             return partial, last
 
         def finish(b, partial, last):
-            total = keep.tile([P, T], F32, name=f"total{b}", tag=f"w2_raw{TURNED - 1 - b}_0")
+            total = keep.tile([P, T], F32, name=f"total{b}", tag=f"picked{BLOCKS - 1}_{TURNED - 1 - b}")
             nc.vector.tensor_tensor(total[:], partial[:].rearrange("p j t -> p (j t)"), last[:], ADD)
             nc.sync.dma_start(out=out[b * P:(b + 1) * P, :], in_=total[:])
 
@@ -210,7 +197,7 @@ def tile_moe_pkd_mlp_relu2_kernel(tc, x_words, x_scales, w1, w2, gate, offs, pos
             gather_scales(e)
         w1_bf = [cast_w1(0, o) for o in range(PASSES)]
         for e in range(E):
-            w1_mx = [quantize(w1_bf[o], H, f"w1_{o}") for o in range(PASSES)]
+            w1_mx = [quantize(w1_bf[o], H, f"w1_{o}", 2) for o in range(PASSES)]
             if e + AHEAD < E:
                 gather_words(e + AHEAD)
             if e > 0:
@@ -219,14 +206,12 @@ def tile_moe_pkd_mlp_relu2_kernel(tc, x_words, x_scales, w1, w2, gate, offs, pos
                 w1_bf = [cast_w1(e + 1, o) for o in range(PASSES)]
             h_bf[e] = first_layer(e, w1_mx)
         turn_gates()
-        w2_bf = [cast_w2(e, 0, "vector") for e in range(2)]
+        w2_bf = [cast_w2(e) for e in range(2)]
         quantize_h(E - 1)
         for e in range(E):
             if e + 2 < E:
-                w2_bf.append(cast_w2(e + 2, 0, "vector"))
-            second_layer(e, 0, quantize(w2_bf[e], P, "w2a"))
-        for e in range(E):
-            second_layer(e, 1, quantize(cast_w2(e, 1, "scalar" if e >= LATE_ON_VECTOR else "vector"), P, "w2b"))
+                w2_bf.append(cast_w2(e + 2))
+            second_layer(e, quantize(w2_bf[e], N, "w2", E))
         parts = [combine(b) for b in range(BLOCKS)]
         for b in range(BLOCKS):
             finish(b, *parts[b])

@@ -103,25 +103,33 @@ def tile_moe_pkd_mlp_relu2_kernel(tc, x_words, x_scales, w1, w2, gate, offs, pos
 
         def cast_w1(e, o):
             grouped = ring.tile([P, H * PACK], BF16, name=f"w1_bf{o}", align_bytes=64)
-            dst = grouped[:].rearrange("p (t m j) -> p m j t", t=PACK, j=PACK)
-            src = w1_raw[e][o][:].rearrange("p j (m t) -> p m j t", t=PACK)
-            split = 0 if e < SCALAR_ALONE else (P, VECTOR_SHARE)[o]
-            if split > 0:
-                nc.vector.tensor_copy(out=dst[:, 0:split], in_=src[:, 0:split])
-            if split < P:
-                nc.scalar.copy(out=dst[:, split:P], in_=src[:, split:P])
+            dst = grouped[:].rearrange("p (u v m j) -> p u m j v", u=2, v=2, j=PACK)
+            src = w1_raw[e][o][:].rearrange("p j (m u v) -> p u m j v", u=2, v=2)
+            if e < SCALAR_ALONE:
+                nc.scalar.copy(out=dst, in_=src)
+            elif o == 0:
+                for u in range(2):
+                    nc.vector.tensor_copy(out=dst[:, u], in_=src[:, u])
+            else:
+                nc.vector.tensor_copy(out=dst[:, :, 0:VECTOR_SHARE], in_=src[:, :, 0:VECTOR_SHARE])
+                nc.scalar.copy(out=dst[:, :, VECTOR_SHARE:P], in_=src[:, :, VECTOR_SHARE:P])
             return grouped
 
         def cast_w2(e):
             grouped = ring.tile([P, N * PACK], BF16, name="w2_bf", align_bytes=64)
-            nc.vector.tensor_copy(out=grouped[:].rearrange("p (c i j) -> p c j i", i=PACK, j=PACK),
-                                  in_=w2_raw[e][:].rearrange("p j (c i) -> p c j i", i=PACK))
+            dst = grouped[:].rearrange("p (b c i j) -> p b c j i", b=BLOCKS, i=PACK, j=PACK)
+            src = w2_raw[e][:].rearrange("p j (b c i) -> p b c j i", b=BLOCKS, i=PACK)
+            for b in range(BLOCKS):
+                nc.vector.tensor_copy(out=dst[:, b], in_=src[:, b])
             return grouped
 
-        def quantize(grouped, width, name, bufs):
+        def quantize(grouped, width, name, bufs, parts):
             codes = ring.tile([P, width], U32, name=f"{name}_codes", align_bytes=64, bufs=bufs)
             scales = ring.tile([P, width], U8, name=f"{name}_scales", align_bytes=64, bufs=bufs)
-            nc.vector.quantize_mx(out=codes[:].bitcast(FP8X4), scales=scales[:], in_=grouped[:])
+            step = width // parts
+            for c in range(0, width, step):
+                nc.vector.quantize_mx(out=codes[:, c:c + step].bitcast(FP8X4), scales=scales[:, c:c + step],
+                                      in_=grouped[:, c * PACK:(c + step) * PACK])
             return codes, scales
 
         def first_layer(e, w1_mx):
@@ -172,17 +180,18 @@ def tile_moe_pkd_mlp_relu2_kernel(tc, x_words, x_scales, w1, w2, gate, offs, pos
                     nc.scalar.activation(out=term[:, j, :], in_=turned[:, j, :], func=ACT.Copy,
                                          scale=gate_cols[:, col:col + 1])
                 scaled.append(term)
-            last = keep.tile([P, T], F32, name=f"last{b}")
-            nc.vector.tensor_tensor(last[:], y[b][:].indirect(pos_t[TOP - 1][:]), gate_last[:], MULT)
             partial = psum_a.tile([P, TOKEN_BLOCKS, P], F32, name="a")
             for j in range(TOKEN_BLOCKS):
                 for r in range(TURNED):
                     nc.tensor.matmul(partial[:, j, :], lhsT=scaled[r][:, j, :], rhs=identity[:], is_transpose=True,
                                      start=(r == 0), stop=(r == TURNED - 1))
-            return partial, last
+            return partial
 
-        def finish(b, partial, last):
-            total = keep.tile([P, T], F32, name=f"total{b}", tag=f"picked{BLOCKS - 1}_{TURNED - 1 - b}")
+        def finish(b, partial):
+            tag = f"picked{BLOCKS - 1}_0" if b == 0 else "last"
+            last = keep.tile([P, T], F32, name=f"last{b}", tag=tag)
+            nc.vector.tensor_tensor(last[:], y[b][:].indirect(pos_t[TOP - 1][:]), gate_last[:], MULT)
+            total = keep.tile([P, T], F32, name=f"total{b}")
             nc.vector.tensor_tensor(total[:], partial[:].rearrange("p j t -> p (j t)"), last[:], ADD)
             nc.sync.dma_start(out=out[b * P:(b + 1) * P, :], in_=total[:])
 
@@ -197,7 +206,7 @@ def tile_moe_pkd_mlp_relu2_kernel(tc, x_words, x_scales, w1, w2, gate, offs, pos
             gather_scales(e)
         w1_bf = [cast_w1(0, o) for o in range(PASSES)]
         for e in range(E):
-            w1_mx = [quantize(w1_bf[o], H, f"w1_{o}", 2) for o in range(PASSES)]
+            w1_mx = [quantize(w1_bf[o], H, f"w1_{o}", 2, 2 if e >= SCALAR_ALONE and o == 0 else 1) for o in range(PASSES)]
             if e + AHEAD < E:
                 gather_words(e + AHEAD)
             if e > 0:
@@ -206,12 +215,9 @@ def tile_moe_pkd_mlp_relu2_kernel(tc, x_words, x_scales, w1, w2, gate, offs, pos
                 w1_bf = [cast_w1(e + 1, o) for o in range(PASSES)]
             h_bf[e] = first_layer(e, w1_mx)
         turn_gates()
-        w2_bf = [cast_w2(e) for e in range(2)]
         quantize_h(E - 1)
         for e in range(E):
-            if e + 2 < E:
-                w2_bf.append(cast_w2(e + 2))
-            second_layer(e, quantize(w2_bf[e], N, "w2", E))
+            second_layer(e, quantize(cast_w2(e), N, "w2", E, BLOCKS))
         parts = [combine(b) for b in range(BLOCKS)]
         for b in range(BLOCKS):
-            finish(b, *parts[b])
+            finish(b, parts[b])

@@ -13,11 +13,14 @@ PASSES = K // K_PASS
 BLOCKS = N // P
 HALVES = C // P
 LIST_COLS = C // 16
+QUADRANTS = P // 32
 TURNED = TOP - 1
 TOKEN_BLOCKS = T // P
+
 AHEAD = 3
 SCALAR_ALONE = 2
-VECTOR_SHARE = 48
+VECTOR_SHARE = 40
+HELD_FROM = 3
 
 FLOPS = 2 * S * (K * H + H * N)
 BYTES = 4 * E * (K * H + H * N) + K * T + K * T // 32 + 4 * TOP * T + 2 * P * (S + TOP * T) // 16 + 4 * N * T
@@ -39,13 +42,14 @@ def tile_moe_pkd_mlp_relu2_kernel(tc, x_words, x_scales, w1, w2, gate, offs, pos
     with ExitStack() as ctx:
         keep = ctx.enter_context(tc.tile_pool(name="keep", bufs=1))
         ring = ctx.enter_context(tc.tile_pool(name="ring", bufs=3))
-        psum_a = ctx.enter_context(tc.psum_pool(name="psum_a", bufs=8))
+        psum = ctx.enter_context(tc.psum_pool(name="psum", bufs=8))
 
         offs_t = keep.tile([P, S // 16], U16, name="offs_t")
         pos_t = [keep.tile([P, T // 16], U16, name=f"pos_t{r}") for r in range(TOP)]
-        xw = [keep.tile([P, T], I32, name=f"xw{o}", align_bytes=64) for o in range(PASSES)]
-        xs = keep.tile([P, T], U8, name="xs", align_bytes=64)
-        w1_raw = [[keep.tile([P, PACK, H], F32, name=f"w1_raw{e}_{o}", align_bytes=64) for o in range(PASSES)] for e in range(E)]
+        token_words = [keep.tile([P, T], I32, name=f"token_words{o}", align_bytes=64) for o in range(PASSES)]
+        token_scales = keep.tile([P, T], U8, name="token_scales", align_bytes=64)
+        w1_raw = [[keep.tile([P, PACK, H], F32, name=f"w1_raw{e}_{o}", align_bytes=64) for o in range(PASSES)]
+                  for e in range(E)]
         w2_raw = [keep.tile([P, PACK, N], F32, name=f"w2_raw{e}") for e in range(E)]
         gate_last = keep.tile([P, T], F32, name="gate_last")
         gate_rows = keep.tile([P, P], F32, name="gate_rows")
@@ -54,35 +58,31 @@ def tile_moe_pkd_mlp_relu2_kernel(tc, x_words, x_scales, w1, w2, gate, offs, pos
         y = [keep.tile([P, S], F32, name=f"y{b}") for b in range(BLOCKS)]
         h_codes = [keep.tile([P, C], U32, name=f"h_codes{e}", align_bytes=64) for e in range(E)]
         h_scales = [keep.tile([P, C], U8, name=f"h_scales{e}", align_bytes=64) for e in range(E)]
-        xg = {}
-        xsg = {}
+        slot_words = {}
+        slot_scales = {}
+        h_bf = {}
 
         def load_w1(e, o):
             rows = w1[e, o * K_PASS:(o + 1) * K_PASS, :]
             nc.sync.dma_start(out=w1_raw[e][o][:], in_=rows.rearrange("(p j) c -> p j c", j=PACK))
 
-        def load_w2(e):
-            nc.sync.dma_start(out=w2_raw[e][:], in_=w2[e].rearrange("(p j) c -> p j c", j=PACK))
-
-        def load_words(o):
-            nc.sync.dma_start(out=xw[o][:], in_=x_words[o].rearrange("p t r -> p (t r)").bitcast(I32))
-
-        nc.vector.memset(xs[:].bitcast(I32), 0)
+        nc.vector.memset(token_scales[:].bitcast(I32), 0)
         nc.gpsimd.memset(gate_rows[:], 0.0)
         make_identity(nc, identity[:])
+
         nc.sync.dma_start(offs_t[:], offs)
-        load_words(0)
-        load_words(1)
+        for o in range(PASSES):
+            nc.sync.dma_start(out=token_words[o][:], in_=x_words[o].rearrange("p t r -> p (t r)").bitcast(I32))
         load_w1(0, 0)
-        for q in range(4):
-            nc.sync.dma_start(out=xs[32 * q:32 * q + 4 * PASSES, :].bitcast(I32),
+        for q in range(QUADRANTS):
+            nc.sync.dma_start(out=token_scales[32 * q:32 * q + 4 * PASSES, :].bitcast(I32),
                               in_=x_scales[:, 4 * q:4 * q + 4, :].bitcast(I32))
         load_w1(0, 1)
         for e in range(1, E):
-            load_w1(e, 0)
-            load_w1(e, 1)
+            for o in range(PASSES):
+                load_w1(e, o)
         for e in range(E):
-            load_w2(e)
+            nc.sync.dma_start(out=w2_raw[e][:], in_=w2[e].rearrange("(p j) c -> p j c", j=PACK))
         for r, pos in enumerate((pos1, pos2, pos3)):
             nc.sync.dma_start(pos_t[r][:], pos)
         nc.sync.dma_start(out=gate_rows[0:TURNED * TOKEN_BLOCKS, :],
@@ -91,15 +91,15 @@ def tile_moe_pkd_mlp_relu2_kernel(tc, x_words, x_scales, w1, w2, gate, offs, pos
 
         def gather_words(e):
             cols = offs_t[:, e * LIST_COLS:(e + 1) * LIST_COLS]
-            tag = f"xg{e}" if e < AHEAD else f"w1_raw{e - AHEAD}_0"
-            xg[e] = keep.tile([P, PASSES, C], U32, name=f"xg{e}", tag=tag, align_bytes=64)
+            tag = f"slot_words{e}" if e < AHEAD else f"w1_raw{e - AHEAD}_0"
+            slot_words[e] = keep.tile([P, PASSES, C], U32, name=f"slot_words{e}", tag=tag, align_bytes=64)
             for o in range(PASSES):
-                nc.vector.tensor_copy(xg[e][:, o, :], xw[o][:].bitcast(U32).indirect(cols))
+                nc.vector.tensor_copy(slot_words[e][:, o, :], token_words[o][:].bitcast(U32).indirect(cols))
 
         def gather_scales(e):
             cols = offs_t[:, e * LIST_COLS:(e + 1) * LIST_COLS]
-            xsg[e] = keep.tile([P, C], U8, name=f"xsg{e}", align_bytes=64)
-            nc.vector.tensor_copy(xsg[e][:], xs[:].indirect(cols))
+            slot_scales[e] = keep.tile([P, C], U8, name=f"slot_scales{e}", align_bytes=64)
+            nc.vector.tensor_copy(slot_scales[e][:], token_scales[:].indirect(cols))
 
         def cast_w1(e, o):
             grouped = ring.tile([P, H * PACK], BF16, name=f"w1_bf{o}", align_bytes=64)
@@ -115,15 +115,16 @@ def tile_moe_pkd_mlp_relu2_kernel(tc, x_words, x_scales, w1, w2, gate, offs, pos
                 nc.scalar.copy(out=dst[:, :, VECTOR_SHARE:P], in_=src[:, :, VECTOR_SHARE:P])
             return grouped
 
-        def cast_w2(e):
-            grouped = ring.tile([P, N * PACK], BF16, name="w2_bf", align_bytes=64)
-            dst = grouped[:].rearrange("p (b c i j) -> p b c j i", b=BLOCKS, i=PACK, j=PACK)
-            src = w2_raw[e][:].rearrange("p j (b c i) -> p b c j i", b=BLOCKS, i=PACK)
-            for b in range(BLOCKS):
-                nc.vector.tensor_copy(out=dst[:, b], in_=src[:, b])
+        def cast_w2(e, b):
+            if (e, b) in ((E - 1, 0), (HELD_FROM, 1)):
+                grouped = keep.tile([P, P * PACK], BF16, name=f"w2_bf{e}_{b}", tag="w2_bf_held", align_bytes=64)
+            else:
+                grouped = ring.tile([P, P * PACK], BF16, name="w2_bf", align_bytes=64, bufs=4)
+            nc.vector.tensor_copy(out=grouped[:].rearrange("p (c i j) -> p c j i", i=PACK, j=PACK),
+                                  in_=w2_raw[e][:, :, b * P:(b + 1) * P].rearrange("p j (c i) -> p c j i", i=PACK))
             return grouped
 
-        def quantize(grouped, width, name, bufs, parts):
+        def quantize_weight(grouped, width, name, bufs, parts):
             codes = ring.tile([P, width], U32, name=f"{name}_codes", align_bytes=64, bufs=bufs)
             scales = ring.tile([P, width], U8, name=f"{name}_scales", align_bytes=64, bufs=bufs)
             step = width // parts
@@ -132,47 +133,54 @@ def tile_moe_pkd_mlp_relu2_kernel(tc, x_words, x_scales, w1, w2, gate, offs, pos
                                       in_=grouped[:, c * PACK:(c + step) * PACK])
             return codes, scales
 
+        def quantize_w1(e, o, grouped):
+            cast_in_halves = e >= SCALAR_ALONE and o == 0
+            return quantize_weight(grouped, H, f"w1_{o}", 2, 2 if cast_in_halves else 1)
+
         def first_layer(e, w1_mx):
-            h_bf = ring.tile([P, C * PACK], BF16, name="h_bf", align_bytes=64)
+            h_bf[e] = ring.tile([P, C * PACK], BF16, name="h_bf", align_bytes=64)
             tag = f"w1_raw{e + 1}_1" if e + 1 < E else "relu_last"
             relu = keep.tile([P, HALVES, P, PACK], F32, name=f"relu{e}", tag=tag, align_bytes=64)
             for half in range(HALVES):
                 slots = slice(half * P, (half + 1) * P)
-                a = psum_a.tile([P, PACK, P], F32, name="a")
+                a = psum.tile([P, PACK, P], F32, name="bank")
                 for t in range(PACK):
                     cols = slice(t * P, (t + 1) * P)
                     for o in range(PASSES):
                         codes, scales = w1_mx[o]
-                        nc.tensor.matmul_mx(out=a[:, t, :], lhsT=codes[:, cols].bitcast(FP8X4), lhsT_scale=scales[:, cols],
-                                            rhs=xg[e][:, o, slots].bitcast(FP8X4), rhs_scale=xsg[e][4 * o:P, slots],
+                        nc.tensor.matmul_mx(out=a[:, t, :], lhsT=codes[:, cols].bitcast(FP8X4),
+                                            lhsT_scale=scales[:, cols],
+                                            rhs=slot_words[e][:, o, slots].bitcast(FP8X4),
+                                            rhs_scale=slot_scales[e][4 * o:P, slots],
                                             start=(o == 0), stop=(o == PASSES - 1))
                 nc.scalar.activation(out=relu[:, half], in_=a[:].rearrange("p t s -> p s t"), func=ACT.Relu)
-                nc.scalar.activation(out=h_bf[:, half * P * PACK:(half + 1) * P * PACK],
+                nc.scalar.activation(out=h_bf[e][:, half * P * PACK:(half + 1) * P * PACK],
                                      in_=relu[:, half].rearrange("p s t -> p (s t)"), func=ACT.Square)
-            return h_bf
 
-        def second_layer(e, w2_mx):
-            codes, scales = w2_mx
-            acc = psum_a.tile([P, BLOCKS, C], F32, name="a")
-            for b in range(BLOCKS):
-                cols = slice(b * P, (b + 1) * P)
-                nc.tensor.matmul_mx(out=acc[:, b, :], lhsT=codes[:, cols].bitcast(FP8X4), lhsT_scale=scales[:, cols],
+        def quantize_h(e):
+            nc.vector.quantize_mx(out=h_codes[e][:].bitcast(FP8X4), scales=h_scales[e][:], in_=h_bf[e][:])
+
+        def second_layer(pairs):
+            w2_bf = [cast_w2(e, b) for e, b in pairs]
+            for (e, b), grouped in zip(pairs, w2_bf):
+                codes, scales = quantize_weight(grouped, P, "w2", E * BLOCKS, 1)
+                acc = psum.tile([P, C], F32, name="bank")
+                nc.tensor.matmul_mx(out=acc[:], lhsT=codes[:].bitcast(FP8X4), lhsT_scale=scales[:],
                                     rhs=h_codes[e][:].bitcast(FP8X4), rhs_scale=h_scales[e][:], start=True, stop=True)
-            for b in range(BLOCKS):
-                nc.scalar.copy(out=y[b][:, e * C:(e + 1) * C], in_=acc[:, b, :])
+                nc.scalar.copy(out=y[b][:, e * C:(e + 1) * C], in_=acc[:])
 
         def turn_gates():
-            turned = psum_a.tile([P, PACK, P], F32, name="a")
+            turned = psum.tile([P, PACK, P], F32, name="bank")
             nc.tensor.transpose(turned[:, 0, :], gate_rows[:], identity[:])
             nc.scalar.copy(out=gate_cols[:], in_=turned[:, 0, 0:TURNED * TOKEN_BLOCKS])
 
-        def combine(b):
+        def sum_turned_choices(b):
             scaled = []
             for r in range(TURNED):
                 picked = keep.tile([P, T], F32, name=f"picked{b}_{r}")
                 nc.vector.tensor_copy(picked[:], y[b][:].indirect(pos_t[r][:]))
-                turned = psum_a.tile([P, TOKEN_BLOCKS, P], F32, name="a")
-                term = ring.tile([P, TOKEN_BLOCKS, P], F32, name="term", bufs=4)
+                turned = psum.tile([P, TOKEN_BLOCKS, P], F32, name="bank")
+                term = ring.tile([P, TOKEN_BLOCKS, P], F32, name="term", bufs=BLOCKS * TURNED)
                 for j in range(TOKEN_BLOCKS):
                     nc.tensor.transpose(turned[:, j, :], picked[:, j * P:(j + 1) * P], identity[:])
                 for j in range(TOKEN_BLOCKS):
@@ -180,14 +188,14 @@ def tile_moe_pkd_mlp_relu2_kernel(tc, x_words, x_scales, w1, w2, gate, offs, pos
                     nc.scalar.activation(out=term[:, j, :], in_=turned[:, j, :], func=ACT.Copy,
                                          scale=gate_cols[:, col:col + 1])
                 scaled.append(term)
-            partial = psum_a.tile([P, TOKEN_BLOCKS, P], F32, name="a")
+            partial = psum.tile([P, TOKEN_BLOCKS, P], F32, name="bank")
             for j in range(TOKEN_BLOCKS):
                 for r in range(TURNED):
                     nc.tensor.matmul(partial[:, j, :], lhsT=scaled[r][:, j, :], rhs=identity[:], is_transpose=True,
                                      start=(r == 0), stop=(r == TURNED - 1))
             return partial
 
-        def finish(b, partial):
+        def add_last_choice(b, partial):
             tag = f"picked{BLOCKS - 1}_0" if b == 0 else "last"
             last = keep.tile([P, T], F32, name=f"last{b}", tag=tag)
             nc.vector.tensor_tensor(last[:], y[b][:].indirect(pos_t[TOP - 1][:]), gate_last[:], MULT)
@@ -195,29 +203,27 @@ def tile_moe_pkd_mlp_relu2_kernel(tc, x_words, x_scales, w1, w2, gate, offs, pos
             nc.vector.tensor_tensor(total[:], partial[:].rearrange("p j t -> p (j t)"), last[:], ADD)
             nc.sync.dma_start(out=out[b * P:(b + 1) * P, :], in_=total[:])
 
-        h_bf = {}
-
-        def quantize_h(e):
-            nc.vector.quantize_mx(out=h_codes[e][:].bitcast(FP8X4), scales=h_scales[e][:], in_=h_bf[e][:])
-
         for e in range(E):
             if e < AHEAD:
                 gather_words(e)
             gather_scales(e)
         w1_bf = [cast_w1(0, o) for o in range(PASSES)]
         for e in range(E):
-            w1_mx = [quantize(w1_bf[o], H, f"w1_{o}", 2, 2 if e >= SCALAR_ALONE and o == 0 else 1) for o in range(PASSES)]
+            w1_mx = [quantize_w1(e, o, w1_bf[o]) for o in range(PASSES)]
             if e + AHEAD < E:
                 gather_words(e + AHEAD)
             if e > 0:
                 quantize_h(e - 1)
             if e + 1 < E:
                 w1_bf = [cast_w1(e + 1, o) for o in range(PASSES)]
-            h_bf[e] = first_layer(e, w1_mx)
+            first_layer(e, w1_mx)
         turn_gates()
         quantize_h(E - 1)
-        for e in range(E):
-            second_layer(e, quantize(cast_w2(e), N, "w2", E, BLOCKS))
-        parts = [combine(b) for b in range(BLOCKS)]
+        for e in range(HELD_FROM):
+            second_layer([(e, b) for b in range(BLOCKS)])
+        for e in range(HELD_FROM, E):
+            second_layer([(e, 0)])
+        second_layer([(e, 1) for e in range(HELD_FROM, E)])
+        partials = [sum_turned_choices(b) for b in range(BLOCKS)]
         for b in range(BLOCKS):
-            finish(b, parts[b])
+            add_last_choice(b, partials[b])

from contextlib import ExitStack

import concourse.mybir as mybir
from concourse.masks import make_identity

K, T, E, C, H, N = 1024, 512, 6, 256, 512, 256
TOP = 3
S = E * C
P = 128
PACK = 4
K_PASS = P * PACK
PASSES = K // K_PASS
BLOCKS = N // P
HALVES = C // P
LIST_COLS = C // 16
QUADRANTS = P // 32
TURNED = TOP - 1
TOKEN_BLOCKS = T // P

AHEAD = 3
SCALAR_ALONE = 2
VECTOR_SHARE = 40
HELD_FROM = 3

FLOPS = 2 * S * (K * H + H * N)
BYTES = 4 * E * (K * H + H * N) + K * T + K * T // 32 + 4 * TOP * T + 2 * P * (S + TOP * T) // 16 + 4 * N * T

F32 = mybir.dt.float32
BF16 = mybir.dt.bfloat16
I32 = mybir.dt.int32
U32 = mybir.dt.uint32
U16 = mybir.dt.uint16
U8 = mybir.dt.uint8
FP8X4 = mybir.dt.float8_e4m3fn_x4
ACT = mybir.ActivationFunctionType
MULT = mybir.AluOpType.mult
ADD = mybir.AluOpType.add


def tile_moe_pkd_mlp_relu2_kernel(tc, x_words, x_scales, w1, w2, gate, offs, pos1, pos2, pos3, out):
    nc = tc.nc
    with ExitStack() as ctx:
        keep = ctx.enter_context(tc.tile_pool(name="keep", bufs=1))
        ring = ctx.enter_context(tc.tile_pool(name="ring", bufs=3))
        psum = ctx.enter_context(tc.psum_pool(name="psum", bufs=8))

        offs_t = keep.tile([P, S // 16], U16, name="offs_t")
        pos_t = [keep.tile([P, T // 16], U16, name=f"pos_t{r}") for r in range(TOP)]
        token_words = [keep.tile([P, T], I32, name=f"token_words{o}", align_bytes=64) for o in range(PASSES)]
        token_scales = keep.tile([P, T], U8, name="token_scales", align_bytes=64)
        w1_raw = [[keep.tile([P, PACK, H], F32, name=f"w1_raw{e}_{o}", align_bytes=64) for o in range(PASSES)]
                  for e in range(E)]
        w2_raw = [keep.tile([P, PACK, N], F32, name=f"w2_raw{e}") for e in range(E)]
        gate_last = keep.tile([P, T], F32, name="gate_last")
        gate_rows = keep.tile([P, P], F32, name="gate_rows")
        gate_cols = keep.tile([P, TURNED * TOKEN_BLOCKS], F32, name="gate_cols")
        identity = keep.tile([P, P], F32, name="identity")
        y = [keep.tile([P, S], F32, name=f"y{b}") for b in range(BLOCKS)]
        h_codes = [keep.tile([P, C], U32, name=f"h_codes{e}", align_bytes=64) for e in range(E)]
        h_scales = [keep.tile([P, C], U8, name=f"h_scales{e}", align_bytes=64) for e in range(E)]
        slot_words = {}
        slot_scales = {}
        h_bf = {}

        def load_w1(e, o):
            rows = w1[e, o * K_PASS:(o + 1) * K_PASS, :]
            nc.sync.dma_start(out=w1_raw[e][o][:], in_=rows.rearrange("(p j) c -> p j c", j=PACK))

        nc.vector.memset(token_scales[:].bitcast(I32), 0)
        nc.gpsimd.memset(gate_rows[:], 0.0)
        make_identity(nc, identity[:])

        nc.sync.dma_start(offs_t[:], offs)
        for o in range(PASSES):
            nc.sync.dma_start(out=token_words[o][:], in_=x_words[o].rearrange("p t r -> p (t r)").bitcast(I32))
        load_w1(0, 0)
        for q in range(QUADRANTS):
            nc.sync.dma_start(out=token_scales[32 * q:32 * q + 4 * PASSES, :].bitcast(I32),
                              in_=x_scales[:, 4 * q:4 * q + 4, :].bitcast(I32))
        load_w1(0, 1)
        for e in range(1, E):
            for o in range(PASSES):
                load_w1(e, o)
        for e in range(E):
            nc.sync.dma_start(out=w2_raw[e][:], in_=w2[e].rearrange("(p j) c -> p j c", j=PACK))
        for r, pos in enumerate((pos1, pos2, pos3)):
            nc.sync.dma_start(pos_t[r][:], pos)
        nc.sync.dma_start(out=gate_rows[0:TURNED * TOKEN_BLOCKS, :],
                          in_=gate[0:TURNED, 0, :].rearrange("r (j p) -> r j p", p=P))
        nc.sync.dma_start(out=gate_last[:], in_=gate[TOP - 1, 0:P, :])

        def gather_words(e):
            cols = offs_t[:, e * LIST_COLS:(e + 1) * LIST_COLS]
            tag = f"slot_words{e}" if e < AHEAD else f"w1_raw{e - AHEAD}_0"
            slot_words[e] = keep.tile([P, PASSES, C], U32, name=f"slot_words{e}", tag=tag, align_bytes=64)
            for o in range(PASSES):
                nc.vector.tensor_copy(slot_words[e][:, o, :], token_words[o][:].bitcast(U32).indirect(cols))

        def gather_scales(e):
            cols = offs_t[:, e * LIST_COLS:(e + 1) * LIST_COLS]
            slot_scales[e] = keep.tile([P, C], U8, name=f"slot_scales{e}", align_bytes=64)
            nc.vector.tensor_copy(slot_scales[e][:], token_scales[:].indirect(cols))

        def cast_w1(e, o):
            grouped = ring.tile([P, H * PACK], BF16, name=f"w1_bf{o}", align_bytes=64)
            dst = grouped[:].rearrange("p (u v m j) -> p u m j v", u=2, v=2, j=PACK)
            src = w1_raw[e][o][:].rearrange("p j (m u v) -> p u m j v", u=2, v=2)
            if e < SCALAR_ALONE:
                nc.scalar.copy(out=dst, in_=src)
            elif o == 0:
                for u in range(2):
                    nc.vector.tensor_copy(out=dst[:, u], in_=src[:, u])
            else:
                nc.vector.tensor_copy(out=dst[:, :, 0:VECTOR_SHARE], in_=src[:, :, 0:VECTOR_SHARE])
                nc.scalar.copy(out=dst[:, :, VECTOR_SHARE:P], in_=src[:, :, VECTOR_SHARE:P])
            return grouped

        def cast_w2(e, b):
            if (e, b) in ((E - 1, 0), (HELD_FROM, 1)):
                grouped = keep.tile([P, P * PACK], BF16, name=f"w2_bf{e}_{b}", tag="w2_bf_held", align_bytes=64)
            else:
                grouped = ring.tile([P, P * PACK], BF16, name="w2_bf", align_bytes=64, bufs=4)
            nc.vector.tensor_copy(out=grouped[:].rearrange("p (c i j) -> p c j i", i=PACK, j=PACK),
                                  in_=w2_raw[e][:, :, b * P:(b + 1) * P].rearrange("p j (c i) -> p c j i", i=PACK))
            return grouped

        def quantize_weight(grouped, width, name, bufs, parts):
            codes = ring.tile([P, width], U32, name=f"{name}_codes", align_bytes=64, bufs=bufs)
            scales = ring.tile([P, width], U8, name=f"{name}_scales", align_bytes=64, bufs=bufs)
            step = width // parts
            for c in range(0, width, step):
                nc.vector.quantize_mx(out=codes[:, c:c + step].bitcast(FP8X4), scales=scales[:, c:c + step],
                                      in_=grouped[:, c * PACK:(c + step) * PACK])
            return codes, scales

        def quantize_w1(e, o, grouped):
            cast_in_halves = e >= SCALAR_ALONE and o == 0
            return quantize_weight(grouped, H, f"w1_{o}", 2, 2 if cast_in_halves else 1)

        def first_layer(e, w1_mx):
            h_bf[e] = ring.tile([P, C * PACK], BF16, name="h_bf", align_bytes=64)
            tag = f"w1_raw{e + 1}_1" if e + 1 < E else "relu_last"
            relu = keep.tile([P, HALVES, P, PACK], F32, name=f"relu{e}", tag=tag, align_bytes=64)
            for half in range(HALVES):
                slots = slice(half * P, (half + 1) * P)
                a = psum.tile([P, PACK, P], F32, name="bank")
                for t in range(PACK):
                    cols = slice(t * P, (t + 1) * P)
                    for o in range(PASSES):
                        codes, scales = w1_mx[o]
                        nc.tensor.matmul_mx(out=a[:, t, :], lhsT=codes[:, cols].bitcast(FP8X4),
                                            lhsT_scale=scales[:, cols],
                                            rhs=slot_words[e][:, o, slots].bitcast(FP8X4),
                                            rhs_scale=slot_scales[e][4 * o:P, slots],
                                            start=(o == 0), stop=(o == PASSES - 1))
                nc.scalar.activation(out=relu[:, half], in_=a[:].rearrange("p t s -> p s t"), func=ACT.Relu)
                nc.scalar.activation(out=h_bf[e][:, half * P * PACK:(half + 1) * P * PACK],
                                     in_=relu[:, half].rearrange("p s t -> p (s t)"), func=ACT.Square)

        def quantize_h(e):
            nc.vector.quantize_mx(out=h_codes[e][:].bitcast(FP8X4), scales=h_scales[e][:], in_=h_bf[e][:])

        def second_layer(pairs):
            w2_bf = [cast_w2(e, b) for e, b in pairs]
            for (e, b), grouped in zip(pairs, w2_bf):
                codes, scales = quantize_weight(grouped, P, "w2", E * BLOCKS, 1)
                acc = psum.tile([P, C], F32, name="bank")
                nc.tensor.matmul_mx(out=acc[:], lhsT=codes[:].bitcast(FP8X4), lhsT_scale=scales[:],
                                    rhs=h_codes[e][:].bitcast(FP8X4), rhs_scale=h_scales[e][:], start=True, stop=True)
                nc.scalar.copy(out=y[b][:, e * C:(e + 1) * C], in_=acc[:])

        def turn_gates():
            turned = psum.tile([P, PACK, P], F32, name="bank")
            nc.tensor.transpose(turned[:, 0, :], gate_rows[:], identity[:])
            nc.scalar.copy(out=gate_cols[:], in_=turned[:, 0, 0:TURNED * TOKEN_BLOCKS])

        def sum_turned_choices(b):
            scaled = []
            for r in range(TURNED):
                picked = keep.tile([P, T], F32, name=f"picked{b}_{r}")
                nc.vector.tensor_copy(picked[:], y[b][:].indirect(pos_t[r][:]))
                turned = psum.tile([P, TOKEN_BLOCKS, P], F32, name="bank")
                term = ring.tile([P, TOKEN_BLOCKS, P], F32, name="term", bufs=BLOCKS * TURNED)
                for j in range(TOKEN_BLOCKS):
                    nc.tensor.transpose(turned[:, j, :], picked[:, j * P:(j + 1) * P], identity[:])
                for j in range(TOKEN_BLOCKS):
                    col = r * TOKEN_BLOCKS + j
                    nc.scalar.activation(out=term[:, j, :], in_=turned[:, j, :], func=ACT.Copy,
                                         scale=gate_cols[:, col:col + 1])
                scaled.append(term)
            partial = psum.tile([P, TOKEN_BLOCKS, P], F32, name="bank")
            for j in range(TOKEN_BLOCKS):
                for r in range(TURNED):
                    nc.tensor.matmul(partial[:, j, :], lhsT=scaled[r][:, j, :], rhs=identity[:], is_transpose=True,
                                     start=(r == 0), stop=(r == TURNED - 1))
            return partial

        def add_last_choice(b, partial):
            tag = f"picked{BLOCKS - 1}_0" if b == 0 else "last"
            last = keep.tile([P, T], F32, name=f"last{b}", tag=tag)
            nc.vector.tensor_tensor(last[:], y[b][:].indirect(pos_t[TOP - 1][:]), gate_last[:], MULT)
            total = keep.tile([P, T], F32, name=f"total{b}")
            nc.vector.tensor_tensor(total[:], partial[:].rearrange("p j t -> p (j t)"), last[:], ADD)
            nc.sync.dma_start(out=out[b * P:(b + 1) * P, :], in_=total[:])

        for e in range(E):
            if e < AHEAD:
                gather_words(e)
            gather_scales(e)
        w1_bf = [cast_w1(0, o) for o in range(PASSES)]
        for e in range(E):
            w1_mx = [quantize_w1(e, o, w1_bf[o]) for o in range(PASSES)]
            if e + AHEAD < E:
                gather_words(e + AHEAD)
            if e > 0:
                quantize_h(e - 1)
            if e + 1 < E:
                w1_bf = [cast_w1(e + 1, o) for o in range(PASSES)]
            first_layer(e, w1_mx)
        turn_gates()
        quantize_h(E - 1)
        for e in range(HELD_FROM):
            second_layer([(e, b) for b in range(BLOCKS)])
        for e in range(HELD_FROM, E):
            second_layer([(e, 0)])
        second_layer([(e, 1) for e in range(HELD_FROM, E)])
        partials = [sum_turned_choices(b) for b in range(BLOCKS)]
        for b in range(BLOCKS):
            add_last_choice(b, partials[b])
